import numpy as np
CORES = [56,61,80,85]
N = 4
def setup_inputs(rng):
    return {"x": rng.standard_normal((N, 128, N * 128), dtype=np.float32)}
def setup_inputs_big(rng):
    d = setup_inputs(rng)
    for k in ("x",): d[k] = (d[k].astype(np.float32) * 1048576.0).astype(d[k].dtype)
    return d
def setup_inputs_small(rng):
    d = setup_inputs(rng)
    for k in ("x",): d[k] = (d[k].astype(np.float32) * (1 / 1048576.0)).astype(d[k].dtype)
    return d
def setup_inputs_apart(rng):
    d = setup_inputs(rng)
    f = (10.0 ** rng.permutation(np.linspace(-1.5, 1.5, N))).astype(np.float32).reshape(N, 1, 1)
    for k in ("x",): d[k] = (d[k].astype(np.float32) * f).astype(d[k].dtype)
    return d
def reference(x):
    X = np.concatenate(list(x), axis=0)
    return {"y": np.stack([X.T[128 * r:128 * r + 128] for r in range(N)])}

@@ -1,0 +1,155 @@
+from concourse.mybir import AluOpType
+
+N = 4
+B = 128
+SIM_CORES = 96
+HOP1_ENGINES = 8
+HOP2_ENGINES = 8
+
+SCRATCH = {
+    "xs": ("sbuf", [B, N * B], "float32"),
+    "ts": ("sbuf", [B, N * B], "float32"),
+    "ident": ("sbuf", [B, B], "float32"),
+    "ps0": ("psum", [B, 512], "float32"),
+    "ps1": ("psum", [B, 512], "float32"),
+    "ps2": ("psum", [B, 512], "float32"),
+    "ps3": ("psum", [B, 512], "float32"),
+    "hold": ("dram", [B, B], "float32"),
+    "land": ("dram", [N, B, B], "float32"),
+}
+SEMAPHORES = (["ones", "idn", "got", "sent"]
+              + ["ld%d" % i for i in range(N)] + ["tp%d" % i for i in range(N)] + ["cp%d" % i for i in range(N)]
+              + ["arr%d" % i for i in range(N)] + ["st%d" % i for i in range(N)])
+
+
+def _pick(mask, n, skip=0):
+    bits = [b for b in range(mask.bit_length()) if (mask >> b) & 1]
+    sel = bits[skip:skip + n]
+    assert len(sel) == n
+    return sum(1 << b for b in sel)
+
+
+def _plan(T, topo):
+    cores = list(T.cores)
+    taken = set(cores)
+    plan = {}
+    for s, cs in enumerate(cores):
+        for d, cd in enumerate(cores):
+            if s == d:
+                continue
+            if topo.may_write(cs, cd):
+                plan[(s, d)] = None
+                continue
+            helper = [k for k in range(SIM_CORES)
+                      if k not in taken and topo.chip(k) == topo.chip(cs) and topo.die(k) == topo.die(cs)
+                      and topo.may_write(cs, k) and topo.may_write(k, cd)][0]
+            taken.add(helper)
+            plan[(s, d)] = helper
+    return plan
+
+
+def _blk(d):
+    return slice(d * B, (d + 1) * B)
+
+
+def _hop1_mask(T, topo, plan, s, d):
+    cs = T.cores[s]
+    far = [e for e in range(N) if e != s and plan[(s, e)] is not None]
+    if plan[(s, d)] is None:
+        return _pick(topo.mask(cs, T.cores[d]), HOP1_ENGINES)
+    return _pick(topo.mask(cs, plan[(s, d)]), HOP1_ENGINES, HOP1_ENGINES * far.index(d))
+
+
+def _count(mask):
+    return bin(mask).count("1")
+
+
+def _send(g, topo, dst, out_ap, in_ap, remote_sem, local_sem, mask):
+    rid, pid, _ = topo.addr(dst)
+    g.remote_dma(out_ap=out_ap, in_ap=in_ap, remote_sem=remote_sem, local_sem=local_sem, pid=pid, routing_id=rid,
+                 dma_engine_mask=mask)
+
+
+def _helper_program(g, core, T, topo, plan):
+    for (s, d), helper in plan.items():
+        if helper != core:
+            continue
+        m2 = _pick(topo.mask(core, T.cores[d]), HOP2_ENGINES)
+        g.wait_ge(T.sem.got, _count(_hop1_mask(T, topo, plan, s, d)))
+        _send(g, topo, T.cores[d], T.land[s], T.hold[:], T.sem["arr%d" % s], T.sem.sent, m2)
+        g.wait_ge(T.sem.sent, _count(m2))
+
+
+def rank_program(g, core, T, topo):
+    plan = _plan(T, topo)
+    r = T.rank_of(core)
+    if r is None:
+        _helper_program(g, core, T, topo, plan)
+        return
+
+    far = [d for d in range(N) if d != r and plan[(r, d)] is not None]
+    near = [d for d in range(N) if d != r and plan[(r, d)] is None]
+    order = far + near + [r]
+
+    g.vector.memset(T.ident[:], 1.0).then_inc(T.sem.ones, 1)
+    g.wait_ge(T.sem.ones, 1)
+    g.affine_select(T.ident[:], T.ident[:], [[-1, B]], AluOpType.is_equal, 0.0, 0, 1).then_inc(T.sem.idn, 1)
+
+    ld_of = {}
+    n_ld = 0
+    for group in (sorted(far), sorted(near + [r])):
+        runs = []
+        for d in group:
+            if runs and runs[-1][-1] == d - 1:
+                runs[-1].append(d)
+            else:
+                runs.append([d])
+        for run in runs:
+            cols = slice(run[0] * B, (run[-1] + 1) * B)
+            g.sync.dma_start(T.xs[:, cols], T.x[:, cols]).then_inc(T.sem["ld%d" % n_ld], 16)
+            for d in run:
+                ld_of[d] = n_ld
+            n_ld += 1
+
+    g.tensor.wait_ge(T.sem.idn, 1)
+    seen = set()
+    for i, d in enumerate(order):
+        if ld_of[d] not in seen:
+            g.tensor.wait_ge(T.sem["ld%d" % ld_of[d]], 16)
+            seen.add(ld_of[d])
+        ps = T["ps%d" % i]
+        g.tensor.transpose(ps[:, 0:B], T.xs[:, _blk(d)], T.ident[:]).then_inc(T.sem["tp%d" % i], 1)
+        g.vector.wait_ge(T.sem["tp%d" % i], 1)
+        g.vector.tensor_copy(T.ts[:, _blk(d)], ps[:, 0:B]).then_inc(T.sem["cp%d" % i], 1)
+
+    sent = 0
+    for i, d in enumerate(order):
+        if d == r:
+            continue
+        m = _hop1_mask(T, topo, plan, r, d)
+        g.wait_ge(T.sem["cp%d" % i], 1)
+        if plan[(r, d)] is None:
+            _send(g, topo, T.cores[d], T.land[r], T.ts[:, _blk(d)], T.sem["arr%d" % r], T.sem.sent, m)
+        else:
+            _send(g, topo, plan[(r, d)], T.hold[:], T.ts[:, _blk(d)], T.sem.got, T.sem.sent, m)
+        sent += _count(m)
+
+    queues = [g.sync, g.scalar]
+    jobs = [(0, r)] + [(1, s) for s in near]
+    jobs += [(k % 2, s) for k, s in enumerate(far)]
+    for q, s in jobs:
+        if s == r:
+            queues[q].wait_ge(T.sem["cp%d" % order.index(r)], 1)
+            src = T.ts[:, _blk(r)]
+        else:
+            if plan[(s, r)] is None:
+                n_in = _count(_hop1_mask(T, topo, plan, s, r))
+            else:
+                n_in = _count(_pick(topo.mask(plan[(s, r)], core), HOP2_ENGINES))
+            queues[q].wait_ge(T.sem["arr%d" % s], n_in)
+            src = T.land[s]
+        queues[q].dma_start(T.y[:, _blk(s)], src).then_inc(T.sem["st%d" % s], 16)
+
+    g.wait_ge(T.sem.sent, sent)
+    for _, s in jobs:
+        g.wait_ge(T.sem["st%d" % s], 16)

@@ -2,6 +2,7 @@ from concourse.mybir import AluOpType
 
 N = 4
 B = 128
+H = B // 2
 SIM_CORES = 96
 HOP1_ENGINES = 8
 HOP2_ENGINES = 8
@@ -14,19 +15,19 @@ SCRATCH = {
     "ps1": ("psum", [B, 512], "float32"),
     "ps2": ("psum", [B, 512], "float32"),
     "ps3": ("psum", [B, 512], "float32"),
-    "hold": ("dram", [B, B], "float32"),
+    "hold": ("dram", [2, B, H], "float32"),
     "land": ("dram", [N, B, B], "float32"),
+    "landh": ("dram", [2 * N, B, H], "float32"),
 }
-SEMAPHORES = (["ones", "idn", "got", "sent"]
-              + ["ld%d" % i for i in range(N)] + ["tp%d" % i for i in range(N)] + ["cp%d" % i for i in range(N)]
-              + ["arr%d" % i for i in range(N)] + ["st%d" % i for i in range(N)])
+SEMAPHORES = (["ones", "idn", "got0", "got1", "sent"]
+              + ["ld%d" % i for i in range(N)] + ["tp%d" % i for i in range(4)] + ["cp%d" % i for i in range(4)]
+              + ["arr%d" % i for i in range(N)] + ["ah%d" % i for i in range(2 * N)] + ["st%d" % i for i in range(5)])
 
 
-def _pick(mask, n, skip=0):
+def _pick(mask, n):
     bits = [b for b in range(mask.bit_length()) if (mask >> b) & 1]
-    sel = bits[skip:skip + n]
-    assert len(sel) == n
-    return sum(1 << b for b in sel)
+    assert len(bits) >= n
+    return sum(1 << b for b in bits[:n])
 
 
 def _plan(T, topo):
@@ -34,30 +35,48 @@ def _plan(T, topo):
     taken = set(cores)
     plan = {}
     for s, cs in enumerate(cores):
-        for d, cd in enumerate(cores):
+        n_far = 0
+        for d, cd in sorted(enumerate(cores), key=lambda e: topo.die(e[1]) != topo.die(cs)):
             if s == d:
                 continue
             if topo.may_write(cs, cd):
                 plan[(s, d)] = None
                 continue
-            helper = [k for k in range(SIM_CORES)
-                      if k not in taken and topo.chip(k) == topo.chip(cs) and topo.die(k) == topo.die(cs)
-                      and topo.may_write(cs, k) and topo.may_write(k, cd)][0]
+            ok = [k for k in range(SIM_CORES)
+                  if k not in taken and topo.die(k) == topo.die(cs) and topo.may_write(cs, k) and topo.may_write(k, cd)]
+            home = [k for k in ok if topo.chip(k) == topo.chip(cs)]
+            away = [k for k in ok if topo.mates(topo.chip(k), topo.chip(cd))
+                    and topo.same_plane(topo.chip(k), topo.chip(cs))]
+            helper = (home, away)[n_far % 2][0]
+            n_far += 1
             taken.add(helper)
             plan[(s, d)] = helper
     return plan
+
+
+def _is_home(T, topo, plan, s, d):
+    return plan[(s, d)] is not None and topo.chip(plan[(s, d)]) == topo.chip(T.cores[s])
 
 
 def _blk(d):
     return slice(d * B, (d + 1) * B)
 
 
+def _half(d, h):
+    return slice(d * B + h * H, d * B + (h + 1) * H)
+
+
 def _hop1_mask(T, topo, plan, s, d):
     cs = T.cores[s]
     far = [e for e in range(N) if e != s and plan[(s, e)] is not None]
-    if plan[(s, d)] is None:
-        return _pick(topo.mask(cs, T.cores[d]), HOP1_ENGINES)
-    return _pick(topo.mask(cs, plan[(s, d)]), HOP1_ENGINES, HOP1_ENGINES * far.index(d))
+    used = 0
+    last = 0
+    for e in sorted(far, key=lambda e: _is_home(T, topo, plan, s, e)):
+        last = _pick(topo.mask(cs, plan[(s, e)]) & ~used, HOP1_ENGINES)
+        if e == d:
+            return last
+        used |= last
+    return last if last else _pick(topo.mask(cs, T.cores[d]), HOP1_ENGINES)
 
 
 def _count(mask):
@@ -70,14 +89,39 @@ def _send(g, topo, dst, out_ap, in_ap, remote_sem, local_sem, mask):
                  dma_engine_mask=mask)
 
 
+def _identity(g, T):
+    g.vector.memset(T.ident[:], 1.0).then_inc(T.sem.ones, 1)
+    g.wait_ge(T.sem.ones, 1)
+    g.affine_select(T.ident[:], T.ident[:], [[-1, B]], AluOpType.is_equal, 0.0, 0, 1).then_inc(T.sem.idn, 1)
+    g.tensor.wait_ge(T.sem.idn, 1)
+
+
+def _turn(g, T, u, rows, in_cols, out_cols):
+    n = rows.stop - rows.start
+    ps = T["ps%d" % u]
+    g.tensor.transpose(ps[:, 0:n], T.xs[rows, in_cols], T.ident[rows, rows]).then_inc(T.sem["tp%d" % u], 1)
+    g.vector.wait_ge(T.sem["tp%d" % u], 1)
+    g.vector.tensor_copy(T.ts[:, out_cols], ps[:, 0:n]).then_inc(T.sem["cp%d" % u], 1)
+
+
 def _helper_program(g, core, T, topo, plan):
     for (s, d), helper in plan.items():
         if helper != core:
             continue
         m2 = _pick(topo.mask(core, T.cores[d]), HOP2_ENGINES)
-        g.wait_ge(T.sem.got, _count(_hop1_mask(T, topo, plan, s, d)))
-        _send(g, topo, T.cores[d], T.land[s], T.hold[:], T.sem["arr%d" % s], T.sem.sent, m2)
-        g.wait_ge(T.sem.sent, _count(m2))
+        n1 = _count(_hop1_mask(T, topo, plan, s, d))
+        if _is_home(T, topo, plan, s, d):
+            _identity(g, T)
+            g.tensor.wait_ge(T.sem.got0, n1)
+            _turn(g, T, 0, slice(0, B), _blk(0), _blk(0))
+            g.wait_ge(T.sem.cp0, 1)
+            _send(g, topo, T.cores[d], T.land[s], T.ts[:, _blk(0)], T.sem["arr%d" % s], T.sem.sent, m2)
+            g.wait_ge(T.sem.sent, _count(m2))
+        else:
+            for h in range(2):
+                g.wait_ge(T.sem["got%d" % h], n1)
+                _send(g, topo, T.cores[d], T.landh[2 * s + h], T.hold[h], T.sem["ah%d" % (2 * s + h)], T.sem.sent, m2)
+            g.wait_ge(T.sem.sent, 2 * _count(m2))
 
 
 def rank_program(g, core, T, topo):
@@ -89,67 +133,66 @@ def rank_program(g, core, T, topo):
 
     far = [d for d in range(N) if d != r and plan[(r, d)] is not None]
     near = [d for d in range(N) if d != r and plan[(r, d)] is None]
-    order = far + near + [r]
+    raw = [d for d in far if _is_home(T, topo, plan, r, d)]
+    cut = [d for d in far if d not in raw]
 
-    g.vector.memset(T.ident[:], 1.0).then_inc(T.sem.ones, 1)
-    g.wait_ge(T.sem.ones, 1)
-    g.affine_select(T.ident[:], T.ident[:], [[-1, B]], AluOpType.is_equal, 0.0, 0, 1).then_inc(T.sem.idn, 1)
-
+    runs = [[d] for d in raw + cut]
+    for d in sorted(near + [r]):
+        if len(runs) > len(far) and runs[-1][-1] == d - 1:
+            runs[-1].append(d)
+        else:
+            runs.append([d])
     ld_of = {}
-    n_ld = 0
-    for group in (sorted(far), sorted(near + [r])):
-        runs = []
-        for d in group:
-            if runs and runs[-1][-1] == d - 1:
-                runs[-1].append(d)
-            else:
-                runs.append([d])
-        for run in runs:
-            cols = slice(run[0] * B, (run[-1] + 1) * B)
-            g.sync.dma_start(T.xs[:, cols], T.x[:, cols]).then_inc(T.sem["ld%d" % n_ld], 16)
-            for d in run:
-                ld_of[d] = n_ld
-            n_ld += 1
+    for k, run in enumerate(runs):
+        cols = slice(run[0] * B, (run[-1] + 1) * B)
+        g.sync.dma_start(T.xs[:, cols], T.x[:, cols]).then_inc(T.sem["ld%d" % k], 16)
+        for d in run:
+            ld_of[d] = k
 
-    g.tensor.wait_ge(T.sem.idn, 1)
+    _identity(g, T)
+
+    units = [(d, slice(h * H, (h + 1) * H), _half(d, h)) for d in cut for h in range(2)]
+    units += [(d, slice(0, B), _blk(d)) for d in near + [r]]
+    assert len(units) <= 4
     seen = set()
-    for i, d in enumerate(order):
+    for u, (d, rows, cols) in enumerate(units):
         if ld_of[d] not in seen:
             g.tensor.wait_ge(T.sem["ld%d" % ld_of[d]], 16)
             seen.add(ld_of[d])
-        ps = T["ps%d" % i]
-        g.tensor.transpose(ps[:, 0:B], T.xs[:, _blk(d)], T.ident[:]).then_inc(T.sem["tp%d" % i], 1)
-        g.vector.wait_ge(T.sem["tp%d" % i], 1)
-        g.vector.tensor_copy(T.ts[:, _blk(d)], ps[:, 0:B]).then_inc(T.sem["cp%d" % i], 1)
+        _turn(g, T, u, rows, _blk(d), cols)
 
     sent = 0
-    for i, d in enumerate(order):
+    for d in raw:
+        m = _hop1_mask(T, topo, plan, r, d)
+        g.wait_ge(T.sem["ld%d" % ld_of[d]], 16)
+        _send(g, topo, plan[(r, d)], T.xs[:, _blk(0)], T.xs[:, _blk(d)], T.sem.got0, T.sem.sent, m)
+        sent += _count(m)
+    for u, (d, rows, cols) in enumerate(units):
         if d == r:
             continue
         m = _hop1_mask(T, topo, plan, r, d)
-        g.wait_ge(T.sem["cp%d" % i], 1)
+        g.wait_ge(T.sem["cp%d" % u], 1)
         if plan[(r, d)] is None:
-            _send(g, topo, T.cores[d], T.land[r], T.ts[:, _blk(d)], T.sem["arr%d" % r], T.sem.sent, m)
+            _send(g, topo, T.cores[d], T.land[r], T.ts[:, cols], T.sem["arr%d" % r], T.sem.sent, m)
         else:
-            _send(g, topo, plan[(r, d)], T.hold[:], T.ts[:, _blk(d)], T.sem.got, T.sem.sent, m)
+            h = rows.start // H
+            _send(g, topo, plan[(r, d)], T.hold[h], T.ts[:, cols], T.sem["got%d" % h], T.sem.sent, m)
         sent += _count(m)
 
-    queues = [g.sync, g.scalar]
-    jobs = [(0, r)] + [(1, s) for s in near]
-    jobs += [(k % 2, s) for k, s in enumerate(far)]
-    for q, s in jobs:
-        if s == r:
-            queues[q].wait_ge(T.sem["cp%d" % order.index(r)], 1)
-            src = T.ts[:, _blk(r)]
+    jobs = [(g.sync, T.sem["cp%d" % (len(units) - 1)], 1, T.ts[:, _blk(r)], _blk(r))]
+    for s in near:
+        jobs.append((g.scalar, T.sem["arr%d" % s], _count(_hop1_mask(T, topo, plan, s, r)), T.land[s], _blk(s)))
+    for s in far:
+        n_in = _count(_pick(topo.mask(plan[(s, r)], core), HOP2_ENGINES))
+        if _is_home(T, topo, plan, s, r):
+            jobs.append((g.sync, T.sem["arr%d" % s], n_in, T.land[s], _blk(s)))
         else:
-            if plan[(s, r)] is None:
-                n_in = _count(_hop1_mask(T, topo, plan, s, r))
-            else:
-                n_in = _count(_pick(topo.mask(plan[(s, r)], core), HOP2_ENGINES))
-            queues[q].wait_ge(T.sem["arr%d" % s], n_in)
-            src = T.land[s]
-        queues[q].dma_start(T.y[:, _blk(s)], src).then_inc(T.sem["st%d" % s], 16)
+            for h in range(2):
+                jobs.append((g.scalar, T.sem["ah%d" % (2 * s + h)], n_in, T.landh[2 * s + h], _half(s, h)))
+    for k, (q, sem, n_in, src, cols) in enumerate(jobs):
+        q.wait_ge(sem, n_in)
+        q.dma_start(T.y[:, cols], src).then_inc(T.sem["st%d" % k], 16)
 
     g.wait_ge(T.sem.sent, sent)
-    for _, s in jobs:
-        g.wait_ge(T.sem["st%d" % s], 16)
+    for k in range(len(jobs)):
+        g.wait_ge(T.sem["st%d" % k], 16)

@@ -1,33 +1,47 @@
+from concourse.bass import DstId, RemoteDMATransfer
 from concourse.mybir import AluOpType
 
 N = 4
 B = 128
-H = B // 2
+L = 2
+M = B - L
 SIM_CORES = 96
-HOP1_ENGINES = 8
+MAIN_ENGINES = 4
+MAIN_ENGINES_OFF = 8
 HOP2_ENGINES = 8
 
 SCRATCH = {
     "xs": ("sbuf", [B, N * B], "float32"),
     "ts": ("sbuf", [B, N * B], "float32"),
+    "ramp": ("sbuf", [B, B], "float32"),
     "ident": ("sbuf", [B, B], "float32"),
     "ps0": ("psum", [B, 512], "float32"),
     "ps1": ("psum", [B, 512], "float32"),
     "ps2": ("psum", [B, 512], "float32"),
     "ps3": ("psum", [B, 512], "float32"),
-    "hold": ("dram", [2, B, H], "float32"),
+    "lead": ("dram", [2 * L, B, 1], "float32"),
+    "holdl": ("dram", [L, B, 1], "float32"),
+    "holdm": ("dram", [B, M], "float32"),
+    "ll": ("sbuf", [B, N * L], "float32"),
+    "landm": ("dram", [N, B, M], "float32"),
     "land": ("dram", [N, B, B], "float32"),
-    "landh": ("dram", [2 * N, B, H], "float32"),
 }
-SEMAPHORES = (["ones", "idn", "got0", "got1", "sent"]
+SEMAPHORES = (["rmp", "idn", "gotl", "gotm", "sent", "lq0", "lq1"]
               + ["ld%d" % i for i in range(N)] + ["tp%d" % i for i in range(4)] + ["cp%d" % i for i in range(4)]
-              + ["arr%d" % i for i in range(N)] + ["ah%d" % i for i in range(2 * N)] + ["st%d" % i for i in range(5)])
+              + ["arr%d" % i for i in range(N)] + ["al%d" % i for i in range(N)] + ["am%d" % i for i in range(N)]
+              + ["st%d" % i for i in range(6)])
 
 
-def _pick(mask, n):
-    bits = [b for b in range(mask.bit_length()) if (mask >> b) & 1]
-    assert len(bits) >= n
-    return sum(1 << b for b in bits[:n])
+def _bits(mask):
+    return [b for b in range(mask.bit_length()) if (mask >> b) & 1]
+
+
+def _to_mask(bits):
+    return sum(1 << b for b in bits)
+
+
+def _count(mask):
+    return len(_bits(mask))
 
 
 def _plan(T, topo):
@@ -58,29 +72,43 @@ def _is_home(T, topo, plan, s, d):
     return plan[(s, d)] is not None and topo.chip(plan[(s, d)]) == topo.chip(T.cores[s])
 
 
+def _far(T, topo, plan, s):
+    return sorted([d for d in range(N) if d != s and plan[(s, d)] is not None],
+                  key=lambda d: _is_home(T, topo, plan, s, d))
+
+
 def _blk(d):
     return slice(d * B, (d + 1) * B)
 
 
-def _half(d, h):
-    return slice(d * B + h * H, d * B + (h + 1) * H)
+def _main_cols(d):
+    return slice(d * B, d * B + M)
 
 
-def _hop1_mask(T, topo, plan, s, d):
+def _lead_cols(d):
+    return slice(d * B + M, (d + 1) * B)
+
+
+def _rank_masks(T, topo, plan, s):
     cs = T.cores[s]
-    far = [e for e in range(N) if e != s and plan[(s, e)] is not None]
     used = 0
-    last = 0
-    for e in sorted(far, key=lambda e: _is_home(T, topo, plan, s, e)):
-        last = _pick(topo.mask(cs, plan[(s, e)]) & ~used, HOP1_ENGINES)
-        if e == d:
-            return last
-        used |= last
-    return last if last else _pick(topo.mask(cs, T.cores[d]), HOP1_ENGINES)
+    res = {}
+    for k, d in enumerate(_far(T, topo, plan, s)):
+        n = MAIN_ENGINES if _is_home(T, topo, plan, s, d) else MAIN_ENGINES_OFF
+        bits = _bits(topo.mask(cs, plan[(s, d)]) & ~used)
+        if k % 2:
+            bits = bits[::-1]
+        if len(bits) >= 2 * n:
+            bits = bits[::2]
+        bits = bits[:n]
+        assert len(bits) == n
+        res[d] = ([1 << b for b in bits[::n // L][:L]], _to_mask(bits))
+        used |= res[d][1]
+    return res
 
 
-def _count(mask):
-    return bin(mask).count("1")
+def _hop2_bits(T, topo, helper, d):
+    return _bits(topo.mask(helper, T.cores[d]))[:HOP2_ENGINES]
 
 
 def _send(g, topo, dst, out_ap, in_ap, remote_sem, local_sem, mask):
@@ -89,17 +117,25 @@ def _send(g, topo, dst, out_ap, in_ap, remote_sem, local_sem, mask):
                  dma_engine_mask=mask)
 
 
+def _send_fused(g, topo, items, local_sem):
+    transfers = []
+    for dst, out_ap, in_ap, remote_sem, mask in items:
+        rid, pid, _ = topo.addr(dst)
+        transfers.append(RemoteDMATransfer(dst_ids=[DstId(rid=rid, pnc=pid)], dma_engine_mask=mask,
+                                           remote_sem=remote_sem, src=in_ap, dst=out_ap))
+    g.remote_dma_fused(transfers, local_sem=local_sem)
+
+
 def _identity(g, T):
-    g.vector.memset(T.ident[:], 1.0).then_inc(T.sem.ones, 1)
-    g.wait_ge(T.sem.ones, 1)
-    g.affine_select(T.ident[:], T.ident[:], [[-1, B]], AluOpType.is_equal, 0.0, 0, 1).then_inc(T.sem.idn, 1)
+    g.iota(T.ramp[:], [[-1, B]], 0, 1, allow_small_or_imprecise_dtypes=True).then_inc(T.sem.rmp, 1)
+    g.vector.wait_ge(T.sem.rmp, 1)
+    g.vector.tensor_scalar(T.ident[:], T.ramp[:], 0.0, None, AluOpType.is_equal).then_inc(T.sem.idn, 1)
     g.tensor.wait_ge(T.sem.idn, 1)
 
 
-def _turn(g, T, u, rows, in_cols, out_cols):
-    n = rows.stop - rows.start
+def _turn(g, T, u, n, in_cols, out_cols):
     ps = T["ps%d" % u]
-    g.tensor.transpose(ps[:, 0:n], T.xs[rows, in_cols], T.ident[rows, rows]).then_inc(T.sem["tp%d" % u], 1)
+    g.tensor.transpose(ps[:, 0:n], T.xs[0:n, in_cols], T.ident[0:n, 0:n]).then_inc(T.sem["tp%d" % u], 1)
     g.vector.wait_ge(T.sem["tp%d" % u], 1)
     g.vector.tensor_copy(T.ts[:, out_cols], ps[:, 0:n]).then_inc(T.sem["cp%d" % u], 1)
 
@@ -108,20 +144,15 @@ def _helper_program(g, core, T, topo, plan):
     for (s, d), helper in plan.items():
         if helper != core:
             continue
-        m2 = _pick(topo.mask(core, T.cores[d]), HOP2_ENGINES)
-        n1 = _count(_hop1_mask(T, topo, plan, s, d))
-        if _is_home(T, topo, plan, s, d):
-            _identity(g, T)
-            g.tensor.wait_ge(T.sem.got0, n1)
-            _turn(g, T, 0, slice(0, B), _blk(0), _blk(0))
-            g.wait_ge(T.sem.cp0, 1)
-            _send(g, topo, T.cores[d], T.land[s], T.ts[:, _blk(0)], T.sem["arr%d" % s], T.sem.sent, m2)
-            g.wait_ge(T.sem.sent, _count(m2))
-        else:
-            for h in range(2):
-                g.wait_ge(T.sem["got%d" % h], n1)
-                _send(g, topo, T.cores[d], T.landh[2 * s + h], T.hold[h], T.sem["ah%d" % (2 * s + h)], T.sem.sent, m2)
-            g.wait_ge(T.sem.sent, 2 * _count(m2))
+        m1 = _rank_masks(T, topo, plan, s)[d]
+        b2 = _hop2_bits(T, topo, core, d)
+        w = len(b2) // L
+        g.wait_ge(T.sem.gotl, L)
+        _send_fused(g, topo, [(T.cores[d], T.ll[:, s * L + i:s * L + i + 1], T.holdl[i], T.sem["al%d" % s],
+                               _to_mask(b2[i * w:(i + 1) * w])) for i in range(L)], T.sem.sent)
+        g.wait_ge(T.sem.gotm, _count(m1[1]))
+        _send(g, topo, T.cores[d], T.landm[s], T.holdm[:], T.sem["am%d" % s], T.sem.sent, _to_mask(b2))
+        g.wait_ge(T.sem.sent, L * w + len(b2))
 
 
 def rank_program(g, core, T, topo):
@@ -131,64 +162,56 @@ def rank_program(g, core, T, topo):
         _helper_program(g, core, T, topo, plan)
         return
 
-    far = [d for d in range(N) if d != r and plan[(r, d)] is not None]
+    far = _far(T, topo, plan, r)
     near = [d for d in range(N) if d != r and plan[(r, d)] is None]
-    raw = [d for d in far if _is_home(T, topo, plan, r, d)]
-    cut = [d for d in far if d not in raw]
+    assert len(far) <= 2
+    masks = _rank_masks(T, topo, plan, r)
+    queues = [g.sync, g.scalar]
 
-    runs = [[d] for d in raw + cut]
-    for d in sorted(near + [r]):
-        if len(runs) > len(far) and runs[-1][-1] == d - 1:
-            runs[-1].append(d)
-        else:
-            runs.append([d])
-    ld_of = {}
-    for k, run in enumerate(runs):
-        cols = slice(run[0] * B, (run[-1] + 1) * B)
-        g.sync.dma_start(T.xs[:, cols], T.x[:, cols]).then_inc(T.sem["ld%d" % k], 16)
-        for d in run:
-            ld_of[d] = k
+    for j, d in enumerate(far):
+        queues[j % 2].dma_start(T.lead[j * L:(j + 1) * L], T.x[M:B, _blk(d)]).then_inc(T.sem["lq%d" % j], 16)
+    for j, d in enumerate(far):
+        queues[j % 2].dma_start(T.xs[0:M, _blk(d)], T.x[0:M, _blk(d)]).then_inc(T.sem["ld%d" % d], 16)
+    for j, d in enumerate(near + [r]):
+        queues[j % 2].dma_start(T.xs[:, _blk(d)], T.x[:, _blk(d)]).then_inc(T.sem["ld%d" % d], 16)
 
     _identity(g, T)
 
-    units = [(d, slice(h * H, (h + 1) * H), _half(d, h)) for d in cut for h in range(2)]
-    units += [(d, slice(0, B), _blk(d)) for d in near + [r]]
+    units = [(d, M, _main_cols(d)) for d in far] + [(d, B, _blk(d)) for d in near + [r]]
     assert len(units) <= 4
-    seen = set()
-    for u, (d, rows, cols) in enumerate(units):
-        if ld_of[d] not in seen:
-            g.tensor.wait_ge(T.sem["ld%d" % ld_of[d]], 16)
-            seen.add(ld_of[d])
-        _turn(g, T, u, rows, _blk(d), cols)
+    for u, (d, n, cols) in enumerate(units):
+        g.tensor.wait_ge(T.sem["ld%d" % d], 16)
+        _turn(g, T, u, n, _blk(d), cols)
 
     sent = 0
-    for d in raw:
-        m = _hop1_mask(T, topo, plan, r, d)
-        g.wait_ge(T.sem["ld%d" % ld_of[d]], 16)
-        _send(g, topo, plan[(r, d)], T.xs[:, _blk(0)], T.xs[:, _blk(d)], T.sem.got0, T.sem.sent, m)
-        sent += _count(m)
-    for u, (d, rows, cols) in enumerate(units):
+    if far:
+        for j in range(len(far)):
+            g.wait_ge(T.sem["lq%d" % j], 16)
+        _send_fused(g, topo, [(plan[(r, d)], T.holdl[i], T.lead[j * L + i], T.sem.gotl, masks[d][0][i])
+                              for j, d in enumerate(far) for i in range(L)], T.sem.sent)
+        sent += len(far) * L
+    for u, (d, n, cols) in enumerate(units):
         if d == r:
             continue
-        m = _hop1_mask(T, topo, plan, r, d)
         g.wait_ge(T.sem["cp%d" % u], 1)
-        if plan[(r, d)] is None:
-            _send(g, topo, T.cores[d], T.land[r], T.ts[:, cols], T.sem["arr%d" % r], T.sem.sent, m)
+        if d in far:
+            m = masks[d][1]
+            _send(g, topo, plan[(r, d)], T.holdm[:], T.ts[:, cols], T.sem.gotm, T.sem.sent, m)
         else:
-            h = rows.start // H
-            _send(g, topo, plan[(r, d)], T.hold[h], T.ts[:, cols], T.sem["got%d" % h], T.sem.sent, m)
+            ok = _bits(topo.mask(core, T.cores[d]))
+            mine = [b for e in far for b in _bits(masks[e][1]) if b in ok and _is_home(T, topo, plan, r, e)]
+            m = _to_mask((mine + [b for b in ok if b not in mine])[:MAIN_ENGINES])
+            _send(g, topo, T.cores[d], T.land[r], T.ts[:, cols], T.sem["arr%d" % r], T.sem.sent, m)
         sent += _count(m)
 
     jobs = [(g.sync, T.sem["cp%d" % (len(units) - 1)], 1, T.ts[:, _blk(r)], _blk(r))]
     for s in near:
-        jobs.append((g.scalar, T.sem["arr%d" % s], _count(_hop1_mask(T, topo, plan, s, r)), T.land[s], _blk(s)))
+        jobs.append((g.scalar, T.sem["arr%d" % s], MAIN_ENGINES, T.land[s], _blk(s)))
     for s in far:
-        n_in = _count(_pick(topo.mask(plan[(s, r)], core), HOP2_ENGINES))
-        if _is_home(T, topo, plan, s, r):
-            jobs.append((g.sync, T.sem["arr%d" % s], n_in, T.land[s], _blk(s)))
-        else:
-            for h in range(2):
-                jobs.append((g.scalar, T.sem["ah%d" % (2 * s + h)], n_in, T.landh[2 * s + h], _half(s, h)))
+        q = g.sync if _is_home(T, topo, plan, s, r) else g.scalar
+        n2 = len(_hop2_bits(T, topo, plan[(s, r)], r))
+        jobs.append((q, T.sem["al%d" % s], (n2 // L) * L, T.ll[:, s * L:(s + 1) * L], _lead_cols(s)))
+        jobs.append((q, T.sem["am%d" % s], n2, T.landm[s], _main_cols(s)))
     for k, (q, sem, n_in, src, cols) in enumerate(jobs):
         q.wait_ge(sem, n_in)
         q.dma_start(T.y[:, cols], src).then_inc(T.sem["st%d" % k], 16)

@@ -3,33 +3,37 @@ from concourse.mybir import AluOpType
 
 N = 4
 B = 128
-L = 2
-M = B - L
+M = B - 1
 SIM_CORES = 96
-MAIN_ENGINES = 4
-MAIN_ENGINES_OFF = 8
+MAIN_ENGINES = 8
 HOP2_ENGINES = 8
+AWAY_CUTS = [0, 64, M]
+HOME_CUTS = [0, 64, M]
+WIDTHS = sorted(set(b - a for cuts in (AWAY_CUTS, HOME_CUTS) for a, b in zip(cuts[:-1], cuts[1:])))
+PIECES = max(len(AWAY_CUTS), len(HOME_CUTS)) - 1
+UNITS = len(AWAY_CUTS) + len(HOME_CUTS) - 2 + 2
 
 SCRATCH = {
-    "xs": ("sbuf", [B, N * B], "float32"),
+    "xs": ("sbuf", [B, UNITS * B], "float32"),
     "ts": ("sbuf", [B, N * B], "float32"),
     "ramp": ("sbuf", [B, B], "float32"),
     "ident": ("sbuf", [B, B], "float32"),
-    "ps0": ("psum", [B, 512], "float32"),
-    "ps1": ("psum", [B, 512], "float32"),
-    "ps2": ("psum", [B, 512], "float32"),
-    "ps3": ("psum", [B, 512], "float32"),
-    "lead": ("dram", [2 * L, B, 1], "float32"),
-    "holdl": ("dram", [L, B, 1], "float32"),
-    "holdm": ("dram", [B, M], "float32"),
-    "ll": ("sbuf", [B, N * L], "float32"),
-    "landm": ("dram", [N, B, M], "float32"),
+    "lead": ("dram", [2, B, 1], "float32"),
+    "holdl": ("dram", [1, B, 1], "float32"),
+    "ll": ("sbuf", [B, 2], "float32"),
     "land": ("dram", [N, B, B], "float32"),
 }
-SEMAPHORES = (["rmp", "idn", "gotl", "gotm", "sent", "lq0", "lq1"]
-              + ["ld%d" % i for i in range(N)] + ["tp%d" % i for i in range(4)] + ["cp%d" % i for i in range(4)]
-              + ["arr%d" % i for i in range(N)] + ["al%d" % i for i in range(N)] + ["am%d" % i for i in range(N)]
-              + ["st%d" % i for i in range(6)])
+for _u in range(UNITS):
+    SCRATCH["ps%d" % _u] = ("psum", [B, 512], "float32")
+for _w in WIDTHS:
+    SCRATCH["hold%d" % _w] = ("dram", [B, _w], "float32")
+    SCRATCH["land%d" % _w] = ("dram", [N, B, _w], "float32")
+SEMAPHORES = (["rmp", "idn", "gotl", "sent", "lq0", "lq1"] + ["gotm%d" % p for p in range(PIECES)]
+              + ["ld%d" % i for i in range(UNITS)] + ["tp%d" % i for i in range(UNITS)]
+              + ["cp%d" % i for i in range(UNITS)]
+              + ["arr%d" % i for i in range(N)] + ["al%d" % i for i in range(N)]
+              + ["am%d_%d" % (p, i) for p in range(PIECES) for i in range(N)]
+              + ["st%d" % i for i in range(UNITS + 1)])
 
 
 def _bits(mask):
@@ -77,33 +81,55 @@ def _far(T, topo, plan, s):
                   key=lambda d: _is_home(T, topo, plan, s, d))
 
 
+def _pieces(T, topo, plan, s, d):
+    cuts = HOME_CUTS if _is_home(T, topo, plan, s, d) else AWAY_CUTS
+    return list(zip(cuts[:-1], cuts[1:]))
+
+
 def _blk(d):
     return slice(d * B, (d + 1) * B)
 
 
-def _main_cols(d):
-    return slice(d * B, d * B + M)
+def _far_sources(plan, d):
+    fs = [s for s in range(N) if s != d and plan[(s, d)] is not None]
+    assert len(fs) == 2 and fs[1] == fs[0] + 1
+    return fs
 
 
-def _lead_cols(d):
-    return slice(d * B + M, (d + 1) * B)
+def _pos(plan, s, d):
+    return _far_sources(plan, d).index(s)
+
+
+def _lead_row(plan, s, d):
+    return B - 1 if _pos(plan, s, d) == 0 else 0
+
+
+def _main_start(plan, s, d):
+    return 0 if _pos(plan, s, d) == 0 else 1
+
+
+def _y_lead_cols(plan, d):
+    fs = _far_sources(plan, d)
+    return slice(fs[0] * B + B - 1, fs[1] * B + 1)
 
 
 def _rank_masks(T, topo, plan, s):
     cs = T.cores[s]
+    far = _far(T, topo, plan, s)
     used = 0
+    own = {}
+    for d in far:
+        bits = _bits(topo.mask(cs, plan[(s, d)]) & ~used)[:MAIN_ENGINES]
+        assert len(bits) == MAIN_ENGINES
+        own[d] = _to_mask(bits)
+        used |= own[d]
     res = {}
-    for k, d in enumerate(_far(T, topo, plan, s)):
-        n = MAIN_ENGINES if _is_home(T, topo, plan, s, d) else MAIN_ENGINES_OFF
-        bits = _bits(topo.mask(cs, plan[(s, d)]) & ~used)
-        if k % 2:
-            bits = bits[::-1]
-        if len(bits) >= 2 * n:
-            bits = bits[::2]
-        bits = bits[:n]
-        assert len(bits) == n
-        res[d] = ([1 << b for b in bits[::n // L][:L]], _to_mask(bits))
-        used |= res[d][1]
+    for d in far:
+        sets = [own[d]]
+        if _is_home(T, topo, plan, s, d):
+            sets += [own[e] for e in far if e != d and own[e] & topo.mask(cs, plan[(s, d)]) == own[e]]
+        n_p = len(_pieces(T, topo, plan, s, d))
+        res[d] = (1 << _bits(own[d])[0], [sets[p % len(sets)] for p in range(n_p)])
     return res
 
 
@@ -133,9 +159,9 @@ def _identity(g, T):
     g.tensor.wait_ge(T.sem.idn, 1)
 
 
-def _turn(g, T, u, n, in_cols, out_cols):
+def _turn(g, T, u, n, out_cols):
     ps = T["ps%d" % u]
-    g.tensor.transpose(ps[:, 0:n], T.xs[0:n, in_cols], T.ident[0:n, 0:n]).then_inc(T.sem["tp%d" % u], 1)
+    g.tensor.transpose(ps[:, 0:n], T.xs[0:n, _blk(u)], T.ident[0:n, 0:n]).then_inc(T.sem["tp%d" % u], 1)
     g.vector.wait_ge(T.sem["tp%d" % u], 1)
     g.vector.tensor_copy(T.ts[:, out_cols], ps[:, 0:n]).then_inc(T.sem["cp%d" % u], 1)
 
@@ -146,13 +172,15 @@ def _helper_program(g, core, T, topo, plan):
             continue
         m1 = _rank_masks(T, topo, plan, s)[d]
         b2 = _hop2_bits(T, topo, core, d)
-        w = len(b2) // L
-        g.wait_ge(T.sem.gotl, L)
-        _send_fused(g, topo, [(T.cores[d], T.ll[:, s * L + i:s * L + i + 1], T.holdl[i], T.sem["al%d" % s],
-                               _to_mask(b2[i * w:(i + 1) * w])) for i in range(L)], T.sem.sent)
-        g.wait_ge(T.sem.gotm, _count(m1[1]))
-        _send(g, topo, T.cores[d], T.landm[s], T.holdm[:], T.sem["am%d" % s], T.sem.sent, _to_mask(b2))
-        g.wait_ge(T.sem.sent, L * w + len(b2))
+        k = _pos(plan, s, d)
+        pieces = _pieces(T, topo, plan, s, d)
+        g.wait_ge(T.sem.gotl, _count(m1[0]))
+        _send(g, topo, T.cores[d], T.ll[:, k:k + 1], T.holdl[0], T.sem["al%d" % s], T.sem.sent, _to_mask(b2))
+        for p, (a, b) in enumerate(pieces):
+            g.wait_ge(T.sem["gotm%d" % p], _count(m1[1][p]))
+            _send(g, topo, T.cores[d], T["land%d" % (b - a)][s], T["hold%d" % (b - a)][:], T.sem["am%d_%d" % (p, s)],
+                  T.sem.sent, _to_mask(b2))
+        g.wait_ge(T.sem.sent, (1 + len(pieces)) * len(b2))
 
 
 def rank_program(g, core, T, topo):
@@ -164,56 +192,63 @@ def rank_program(g, core, T, topo):
 
     far = _far(T, topo, plan, r)
     near = [d for d in range(N) if d != r and plan[(r, d)] is None]
-    assert len(far) <= 2
+    assert len(far) == 2 and len(near) == 1
     masks = _rank_masks(T, topo, plan, r)
     queues = [g.sync, g.scalar]
 
+    units = []
     for j, d in enumerate(far):
-        queues[j % 2].dma_start(T.lead[j * L:(j + 1) * L], T.x[M:B, _blk(d)]).then_inc(T.sem["lq%d" % j], 16)
+        for p, (a, b) in enumerate(_pieces(T, topo, plan, r, d)):
+            units.append((d, p, _main_start(plan, r, d) + a, b - a, slice(d * B + a, d * B + b), j % 2))
+    units.append((near[0], 0, 0, B, _blk(near[0]), 1))
+    units.append((r, 0, 0, B, _blk(r), 0))
+    assert len(units) == UNITS
+
     for j, d in enumerate(far):
-        queues[j % 2].dma_start(T.xs[0:M, _blk(d)], T.x[0:M, _blk(d)]).then_inc(T.sem["ld%d" % d], 16)
-    for j, d in enumerate(near + [r]):
-        queues[j % 2].dma_start(T.xs[:, _blk(d)], T.x[:, _blk(d)]).then_inc(T.sem["ld%d" % d], 16)
+        i = _lead_row(plan, r, d)
+        queues[j % 2].dma_start(T.lead[j:j + 1], T.x[i:i + 1, _blk(d)]).then_inc(T.sem["lq%d" % j], 16)
+    for u, (d, p, i, n, cols, q) in enumerate(units):
+        queues[q].dma_start(T.xs[0:n, _blk(u)], T.x[i:i + n, _blk(d)]).then_inc(T.sem["ld%d" % u], 16)
 
     _identity(g, T)
 
-    units = [(d, M, _main_cols(d)) for d in far] + [(d, B, _blk(d)) for d in near + [r]]
-    assert len(units) <= 4
-    for u, (d, n, cols) in enumerate(units):
-        g.tensor.wait_ge(T.sem["ld%d" % d], 16)
-        _turn(g, T, u, n, _blk(d), cols)
+    for u, (d, p, i, n, cols, q) in enumerate(units):
+        g.tensor.wait_ge(T.sem["ld%d" % u], 16)
+        _turn(g, T, u, n, cols)
 
     sent = 0
-    if far:
-        for j in range(len(far)):
-            g.wait_ge(T.sem["lq%d" % j], 16)
-        _send_fused(g, topo, [(plan[(r, d)], T.holdl[i], T.lead[j * L + i], T.sem.gotl, masks[d][0][i])
-                              for j, d in enumerate(far) for i in range(L)], T.sem.sent)
-        sent += len(far) * L
-    for u, (d, n, cols) in enumerate(units):
+    for j in range(len(far)):
+        g.wait_ge(T.sem["lq%d" % j], 16)
+    _send_fused(g, topo, [(plan[(r, d)], T.holdl[0], T.lead[j], T.sem.gotl, masks[d][0])
+                          for j, d in enumerate(far)], T.sem.sent)
+    sent += len(far)
+    near_mask = [masks[e][1][0] for e in far if _is_home(T, topo, plan, r, e)][0]
+    for u, (d, p, i, n, cols, q) in enumerate(units):
         if d == r:
             continue
         g.wait_ge(T.sem["cp%d" % u], 1)
         if d in far:
-            m = masks[d][1]
-            _send(g, topo, plan[(r, d)], T.holdm[:], T.ts[:, cols], T.sem.gotm, T.sem.sent, m)
+            m = masks[d][1][p]
+            _send(g, topo, plan[(r, d)], T["hold%d" % n][:], T.ts[:, cols], T.sem["gotm%d" % p], T.sem.sent, m)
         else:
-            ok = _bits(topo.mask(core, T.cores[d]))
-            mine = [b for e in far for b in _bits(masks[e][1]) if b in ok and _is_home(T, topo, plan, r, e)]
-            m = _to_mask((mine + [b for b in ok if b not in mine])[:MAIN_ENGINES])
+            m = near_mask
+            assert m & topo.mask(core, T.cores[d]) == m
             _send(g, topo, T.cores[d], T.land[r], T.ts[:, cols], T.sem["arr%d" % r], T.sem.sent, m)
         sent += _count(m)
 
-    jobs = [(g.sync, T.sem["cp%d" % (len(units) - 1)], 1, T.ts[:, _blk(r)], _blk(r))]
+    jobs = [(g.sync, [(T.sem["cp%d" % (UNITS - 1)], 1)], T.ts[:, _blk(r)], _blk(r))]
     for s in near:
-        jobs.append((g.scalar, T.sem["arr%d" % s], MAIN_ENGINES, T.land[s], _blk(s)))
+        jobs.append((g.scalar, [(T.sem["arr%d" % s], MAIN_ENGINES)], T.land[s], _blk(s)))
+    n2 = {s: len(_hop2_bits(T, topo, plan[(s, r)], r)) for s in far}
+    jobs.append((g.scalar, [(T.sem["al%d" % s], n2[s]) for s in far], T.ll[:], _y_lead_cols(plan, r)))
     for s in far:
         q = g.sync if _is_home(T, topo, plan, s, r) else g.scalar
-        n2 = len(_hop2_bits(T, topo, plan[(s, r)], r))
-        jobs.append((q, T.sem["al%d" % s], (n2 // L) * L, T.ll[:, s * L:(s + 1) * L], _lead_cols(s)))
-        jobs.append((q, T.sem["am%d" % s], n2, T.landm[s], _main_cols(s)))
-    for k, (q, sem, n_in, src, cols) in enumerate(jobs):
-        q.wait_ge(sem, n_in)
+        c0 = s * B + _main_start(plan, s, r)
+        for p, (a, b) in enumerate(_pieces(T, topo, plan, s, r)):
+            jobs.append((q, [(T.sem["am%d_%d" % (p, s)], n2[s])], T["land%d" % (b - a)][s], slice(c0 + a, c0 + b)))
+    for k, (q, waits, src, cols) in enumerate(jobs):
+        for sem, n_in in waits:
+            q.wait_ge(sem, n_in)
         q.dma_start(T.y[:, cols], src).then_inc(T.sem["st%d" % k], 16)
 
     g.wait_ge(T.sem.sent, sent)

from concourse.bass import DstId, RemoteDMATransfer
from concourse.mybir import AluOpType

N = 4
B = 128
M = B - 1
SIM_CORES = 96
MAIN_ENGINES = 8
HOP2_ENGINES = 8
AWAY_CUTS = [0, 64, M]
HOME_CUTS = [0, 64, M]
WIDTHS = sorted(set(b - a for cuts in (AWAY_CUTS, HOME_CUTS) for a, b in zip(cuts[:-1], cuts[1:])))
PIECES = max(len(AWAY_CUTS), len(HOME_CUTS)) - 1
UNITS = len(AWAY_CUTS) + len(HOME_CUTS) - 2 + 2

SCRATCH = {
    "xs": ("sbuf", [B, UNITS * B], "float32"),
    "ts": ("sbuf", [B, N * B], "float32"),
    "ramp": ("sbuf", [B, B], "float32"),
    "ident": ("sbuf", [B, B], "float32"),
    "lead": ("dram", [2, B, 1], "float32"),
    "holdl": ("dram", [1, B, 1], "float32"),
    "ll": ("sbuf", [B, 2], "float32"),
    "land": ("dram", [N, B, B], "float32"),
}
for _u in range(UNITS):
    SCRATCH["ps%d" % _u] = ("psum", [B, 512], "float32")
for _w in WIDTHS:
    SCRATCH["hold%d" % _w] = ("dram", [B, _w], "float32")
    SCRATCH["land%d" % _w] = ("dram", [N, B, _w], "float32")
SEMAPHORES = (["rmp", "idn", "gotl", "sent", "lq0", "lq1"] + ["gotm%d" % p for p in range(PIECES)]
              + ["ld%d" % i for i in range(UNITS)] + ["tp%d" % i for i in range(UNITS)]
              + ["cp%d" % i for i in range(UNITS)]
              + ["arr%d" % i for i in range(N)] + ["al%d" % i for i in range(N)]
              + ["am%d_%d" % (p, i) for p in range(PIECES) for i in range(N)]
              + ["st%d" % i for i in range(UNITS + 1)])


def _bits(mask):
    return [b for b in range(mask.bit_length()) if (mask >> b) & 1]


def _to_mask(bits):
    return sum(1 << b for b in bits)


def _count(mask):
    return len(_bits(mask))


def _plan(T, topo):
    cores = list(T.cores)
    taken = set(cores)
    plan = {}
    for s, cs in enumerate(cores):
        n_far = 0
        for d, cd in sorted(enumerate(cores), key=lambda e: topo.die(e[1]) != topo.die(cs)):
            if s == d:
                continue
            if topo.may_write(cs, cd):
                plan[(s, d)] = None
                continue
            ok = [k for k in range(SIM_CORES)
                  if k not in taken and topo.die(k) == topo.die(cs) and topo.may_write(cs, k) and topo.may_write(k, cd)]
            home = [k for k in ok if topo.chip(k) == topo.chip(cs)]
            away = [k for k in ok if topo.mates(topo.chip(k), topo.chip(cd))
                    and topo.same_plane(topo.chip(k), topo.chip(cs))]
            helper = (home, away)[n_far % 2][0]
            n_far += 1
            taken.add(helper)
            plan[(s, d)] = helper
    return plan


def _is_home(T, topo, plan, s, d):
    return plan[(s, d)] is not None and topo.chip(plan[(s, d)]) == topo.chip(T.cores[s])


def _far(T, topo, plan, s):
    return sorted([d for d in range(N) if d != s and plan[(s, d)] is not None],
                  key=lambda d: _is_home(T, topo, plan, s, d))


def _pieces(T, topo, plan, s, d):
    cuts = HOME_CUTS if _is_home(T, topo, plan, s, d) else AWAY_CUTS
    return list(zip(cuts[:-1], cuts[1:]))


def _blk(d):
    return slice(d * B, (d + 1) * B)


def _far_sources(plan, d):
    fs = [s for s in range(N) if s != d and plan[(s, d)] is not None]
    assert len(fs) == 2 and fs[1] == fs[0] + 1
    return fs


def _pos(plan, s, d):
    return _far_sources(plan, d).index(s)


def _lead_row(plan, s, d):
    return B - 1 if _pos(plan, s, d) == 0 else 0


def _main_start(plan, s, d):
    return 0 if _pos(plan, s, d) == 0 else 1


def _y_lead_cols(plan, d):
    fs = _far_sources(plan, d)
    return slice(fs[0] * B + B - 1, fs[1] * B + 1)


def _rank_masks(T, topo, plan, s):
    cs = T.cores[s]
    far = _far(T, topo, plan, s)
    used = 0
    own = {}
    for d in far:
        bits = _bits(topo.mask(cs, plan[(s, d)]) & ~used)[:MAIN_ENGINES]
        assert len(bits) == MAIN_ENGINES
        own[d] = _to_mask(bits)
        used |= own[d]
    res = {}
    for d in far:
        sets = [own[d]]
        if _is_home(T, topo, plan, s, d):
            sets += [own[e] for e in far if e != d and own[e] & topo.mask(cs, plan[(s, d)]) == own[e]]
        n_p = len(_pieces(T, topo, plan, s, d))
        res[d] = (1 << _bits(own[d])[0], [sets[p % len(sets)] for p in range(n_p)])
    return res


def _hop2_bits(T, topo, helper, d):
    return _bits(topo.mask(helper, T.cores[d]))[:HOP2_ENGINES]


def _send(g, topo, dst, out_ap, in_ap, remote_sem, local_sem, mask):
    rid, pid, _ = topo.addr(dst)
    g.remote_dma(out_ap=out_ap, in_ap=in_ap, remote_sem=remote_sem, local_sem=local_sem, pid=pid, routing_id=rid,
                 dma_engine_mask=mask)


def _send_fused(g, topo, items, local_sem):
    transfers = []
    for dst, out_ap, in_ap, remote_sem, mask in items:
        rid, pid, _ = topo.addr(dst)
        transfers.append(RemoteDMATransfer(dst_ids=[DstId(rid=rid, pnc=pid)], dma_engine_mask=mask,
                                           remote_sem=remote_sem, src=in_ap, dst=out_ap))
    g.remote_dma_fused(transfers, local_sem=local_sem)


def _identity(g, T):
    g.iota(T.ramp[:], [[-1, B]], 0, 1, allow_small_or_imprecise_dtypes=True).then_inc(T.sem.rmp, 1)
    g.vector.wait_ge(T.sem.rmp, 1)
    g.vector.tensor_scalar(T.ident[:], T.ramp[:], 0.0, None, AluOpType.is_equal).then_inc(T.sem.idn, 1)
    g.tensor.wait_ge(T.sem.idn, 1)


def _turn(g, T, u, n, out_cols):
    ps = T["ps%d" % u]
    g.tensor.transpose(ps[:, 0:n], T.xs[0:n, _blk(u)], T.ident[0:n, 0:n]).then_inc(T.sem["tp%d" % u], 1)
    g.vector.wait_ge(T.sem["tp%d" % u], 1)
    g.vector.tensor_copy(T.ts[:, out_cols], ps[:, 0:n]).then_inc(T.sem["cp%d" % u], 1)


def _helper_program(g, core, T, topo, plan):
    for (s, d), helper in plan.items():
        if helper != core:
            continue
        m1 = _rank_masks(T, topo, plan, s)[d]
        b2 = _hop2_bits(T, topo, core, d)
        k = _pos(plan, s, d)
        pieces = _pieces(T, topo, plan, s, d)
        g.wait_ge(T.sem.gotl, _count(m1[0]))
        _send(g, topo, T.cores[d], T.ll[:, k:k + 1], T.holdl[0], T.sem["al%d" % s], T.sem.sent, _to_mask(b2))
        for p, (a, b) in enumerate(pieces):
            g.wait_ge(T.sem["gotm%d" % p], _count(m1[1][p]))
            _send(g, topo, T.cores[d], T["land%d" % (b - a)][s], T["hold%d" % (b - a)][:], T.sem["am%d_%d" % (p, s)],
                  T.sem.sent, _to_mask(b2))
        g.wait_ge(T.sem.sent, (1 + len(pieces)) * len(b2))


def rank_program(g, core, T, topo):
    plan = _plan(T, topo)
    r = T.rank_of(core)
    if r is None:
        _helper_program(g, core, T, topo, plan)
        return

    far = _far(T, topo, plan, r)
    near = [d for d in range(N) if d != r and plan[(r, d)] is None]
    assert len(far) == 2 and len(near) == 1
    masks = _rank_masks(T, topo, plan, r)
    queues = [g.sync, g.scalar]

    units = []
    for j, d in enumerate(far):
        for p, (a, b) in enumerate(_pieces(T, topo, plan, r, d)):
            units.append((d, p, _main_start(plan, r, d) + a, b - a, slice(d * B + a, d * B + b), j % 2))
    units.append((near[0], 0, 0, B, _blk(near[0]), 1))
    units.append((r, 0, 0, B, _blk(r), 0))
    assert len(units) == UNITS

    for j, d in enumerate(far):
        i = _lead_row(plan, r, d)
        queues[j % 2].dma_start(T.lead[j:j + 1], T.x[i:i + 1, _blk(d)]).then_inc(T.sem["lq%d" % j], 16)
    for u, (d, p, i, n, cols, q) in enumerate(units):
        queues[q].dma_start(T.xs[0:n, _blk(u)], T.x[i:i + n, _blk(d)]).then_inc(T.sem["ld%d" % u], 16)

    _identity(g, T)

    for u, (d, p, i, n, cols, q) in enumerate(units):
        g.tensor.wait_ge(T.sem["ld%d" % u], 16)
        _turn(g, T, u, n, cols)

    sent = 0
    for j in range(len(far)):
        g.wait_ge(T.sem["lq%d" % j], 16)
    _send_fused(g, topo, [(plan[(r, d)], T.holdl[0], T.lead[j], T.sem.gotl, masks[d][0])
                          for j, d in enumerate(far)], T.sem.sent)
    sent += len(far)
    near_mask = [masks[e][1][0] for e in far if _is_home(T, topo, plan, r, e)][0]
    for u, (d, p, i, n, cols, q) in enumerate(units):
        if d == r:
            continue
        g.wait_ge(T.sem["cp%d" % u], 1)
        if d in far:
            m = masks[d][1][p]
            _send(g, topo, plan[(r, d)], T["hold%d" % n][:], T.ts[:, cols], T.sem["gotm%d" % p], T.sem.sent, m)
        else:
            m = near_mask
            assert m & topo.mask(core, T.cores[d]) == m
            _send(g, topo, T.cores[d], T.land[r], T.ts[:, cols], T.sem["arr%d" % r], T.sem.sent, m)
        sent += _count(m)

    jobs = [(g.sync, [(T.sem["cp%d" % (UNITS - 1)], 1)], T.ts[:, _blk(r)], _blk(r))]
    for s in near:
        jobs.append((g.scalar, [(T.sem["arr%d" % s], MAIN_ENGINES)], T.land[s], _blk(s)))
    n2 = {s: len(_hop2_bits(T, topo, plan[(s, r)], r)) for s in far}
    jobs.append((g.scalar, [(T.sem["al%d" % s], n2[s]) for s in far], T.ll[:], _y_lead_cols(plan, r)))
    for s in far:
        q = g.sync if _is_home(T, topo, plan, s, r) else g.scalar
        c0 = s * B + _main_start(plan, s, r)
        for p, (a, b) in enumerate(_pieces(T, topo, plan, s, r)):
            jobs.append((q, [(T.sem["am%d_%d" % (p, s)], n2[s])], T["land%d" % (b - a)][s], slice(c0 + a, c0 + b)))
    for k, (q, waits, src, cols) in enumerate(jobs):
        for sem, n_in in waits:
            q.wait_ge(sem, n_in)
        q.dma_start(T.y[:, cols], src).then_inc(T.sem["st%d" % k], 16)

    g.wait_ge(T.sem.sent, sent)
    for k in range(len(jobs)):
        g.wait_ge(T.sem["st%d" % k], 16)
